import numpy as np, ml_dtypes
CORES = [3,11,19,27,35,43,51,59]
N = 8
BF = ml_dtypes.bfloat16
V, S, P, Q = 1, 2048, 64, 512
def fill(rng, l, cap):
    l = np.minimum(l, cap); e = S - int(np.sum(l)); o = rng.permutation(P); room = (cap - l)[o]; before = np.add.accumulate(room) - room
    l[o] += np.clip(e - before, 0, room); return l
def lens(rng, cap, g):
    c = np.sort(rng.permutation(S - 1)[:P - 1]) + 1
    return fill(rng, np.diff(np.concatenate([[0], c, [S]])), cap)
def put(d, v, g, a, l):
    j = v % V * P; d["frm"][v // V, g, j:j + P] = a; d["ln"][v // V, g, j:j + P] = l
def make(rng, lengths, share):
    d = {"frm": np.zeros((N, 8, V * P), np.int32), "ln": np.zeros((N, 8, V * P), np.int32), "lit": rng.integers(0, 256, (N, 8, Q)).astype(np.int32)}
    for v in range(N * V):
        for g in range(8):
            s = 1.0 if v == 0 else share[v, g]
            l = lengths(rng, Q if s == 1 else S, g); new = (rng.random(P) < s) & (l <= Q)
            put(d, v, g, np.where(new, S + rng.integers(0, np.maximum(Q - l, 0) + 1), rng.integers(0, S - l + 1)), l)
    return d
def setup_inputs(rng):
    return make(rng, lens, np.full((N * V, 8), 0.25))
def setup_inputs_long(rng):
    def lengths(rng, cap, g):
        l = fill(rng, np.ones(P, np.int64), cap)
        return np.sort(l)[::-1].copy() if g == 0 else np.sort(l) if g == 7 else l
    return make(rng, lengths, np.full((N * V, 8), 0.25))
def setup_inputs_ends(rng):
    d = make(rng, lambda rng, cap, g: np.full(P, S // P), np.full((N * V, 8), 0.25))
    k = rng.integers(0, 3, d["frm"].shape); new = d["frm"] >= S
    d["frm"] = np.where(k == 0, np.where(new, S, 0), np.where(k == 1, np.where(new, S + Q, S) - d["ln"], d["frm"])).astype(np.int32)
    return d
def setup_inputs_moves(rng):
    d = setup_inputs(rng)
    for v in range(1, N * V):
        for g in range(8):
            l = lens(rng, S, g); c = np.add.accumulate(l) - l; p = np.arange(P) if g == v % 8 else rng.permutation(P)
            put(d, v, g, c[p], l[p])
    return d
def setup_inputs_spread(rng):
    share = rng.choice(np.array([0, 0.125, 0.5, 1]), (N * V, 8)); share[N * V - 1, 0] = 0; share[N * V - 1, 1] = 1
    d = make(rng, lambda rng, cap, g: fill(rng, 1 + rng.multinomial(S - P, rng.dirichlet(np.full(P, 0.125))), cap), share)
    d["lit"] = np.where(rng.random(d["lit"].shape) < 0.5, 255 * rng.integers(0, 2, d["lit"].shape), d["lit"]).astype(np.int32)
    return d
def check_inputs(d):
    bad = []; a = np.asarray(d["frm"]).astype(np.int64).reshape(N, 8, V, P); l = np.asarray(d["ln"]).astype(np.int64).reshape(N, 8, V, P); t = np.asarray(d["lit"])
    if (l < 1).any() or (np.sum(l, axis=3) != S).any(): bad.append("lengths")
    copied = (a >= 0) & (a + l <= S); new = (a >= S) & (a + l <= S + Q)
    if not (copied | new).all(): bad.append("pieces")
    if not new[0, :, 0].all(): bad.append("version 0")
    if (t < 0).any() or (t > 255).any(): bad.append("literals")
    return bad
def reference(frm, ln, lit):
    y = np.zeros((N, 8, V * S), np.float32); old = np.zeros((8, S), np.int64)
    for v in range(N * V):
        r, k = v // V, v % V; src = np.concatenate([old, lit[r]], axis=1); new = np.zeros((8, S), np.int64)
        for g in range(8):
            a = frm[r, g, k * P:(k + 1) * P]; l = ln[r, g, k * P:(k + 1) * P]; first = np.add.accumulate(l) - l
            new[g] = src[g][np.repeat(a - first, l) + np.arange(S)]
        y[r, :, k * S:(k + 1) * S] = new; old = new
    return {"y": y}

@@ -1,0 +1,251 @@
+from concourse.bass import DstId, RemoteDMATransfer
+from concourse.mybir import dt, AluOpType, AxisListType, ActivationFunctionType
+
+NV = 8
+S = 2048
+Q = 512
+HALF = S // 2
+BW = 136
+
+SCRATCH = {
+    "lni": ("sbuf", [128, 64], "int32"),
+    "fri": ("sbuf", [128, 64], "int32"),
+    "liti": ("sbuf", [128, 32], "int32"),
+    "litb": ("sbuf", [128, 32], "bfloat16"),
+    "lnf": ("sbuf", [128, 64], "float32"),
+    "zf": ("sbuf", [128, 64], "float32"),
+    "stf": ("sbuf", [128, 72], "float32"),
+    "sti": ("sbuf", [128, 64], "int32"),
+    "smi": ("sbuf", [128, 64], "int32"),
+    "sqi": ("sbuf", [128, 64], "int32"),
+    "exi": ("sbuf", [128, 72], "int32"),
+    "dlt": ("sbuf", [128, 64], "float32"),
+    "xm": ("sbuf", [128, 192], "bfloat16"),
+    "xq": ("sbuf", [128, 192], "bfloat16"),
+    "xh": ("sbuf", [128, 192], "bfloat16"),
+    "xl": ("sbuf", [128, 192], "bfloat16"),
+    "iom": ("sbuf", [128, 136], "bfloat16"),
+    "qm1": ("sbuf", [128, 32], "bfloat16"),
+    "qm2": ("sbuf", [128, 32], "bfloat16"),
+    "one": ("sbuf", [128, 128], "bfloat16"),
+    "sele": ("sbuf", [128, 8], "bfloat16"),
+    "selo": ("sbuf", [128, 8], "bfloat16"),
+    "c16": ("sbuf", [128, 128], "bfloat16"),
+    "cneg": ("sbuf", [128, 128], "bfloat16"),
+    "qrow": ("sbuf", [128, 128], "bfloat16"),
+    "bcol": ("sbuf", [128, 4], "float32"),
+    "sgn": ("sbuf", [128, 128], "bfloat16"),
+    "ap": ("sbuf", [128, 512], "bfloat16"),
+    "am": ("sbuf", [128, 512], "bfloat16"),
+    "bh": ("sbuf", [128, 4 * BW], "bfloat16"),
+    "bl": ("sbuf", [128, 4 * BW], "bfloat16"),
+    "wl": ("sbuf", [128, Q], "bfloat16"),
+    "yo": ("sbuf", [128, S], "float32"),
+    "lland": ("dram", [NV, 128, 32], "bfloat16"),
+    "psm": ("psum", [128, 512], "float32"),
+    "psq": ("psum", [128, 512], "float32"),
+    "pdh": ("psum", [128, 512], "float32"),
+    "pdl": ("psum", [128, 512], "float32"),
+    "pout": ("psum", [128, 512], "float32"),
+}
+for _v in range(NV):
+    SCRATCH["ls%d" % _v] = ("sbuf", [128, 128], "uint16")
+for _v in range(NV - 1):
+    SCRATCH["w%d" % _v] = ("sbuf", [128, S + Q], "bfloat16")
+
+NOPS = 100
+SEMAPHORES = (["d_ln", "d_fr", "d_li", "d_y0", "d_y1", "loc_k", "loc_l"]
+              + ["arrk%d" % v for v in range(NV)] + ["arrl%d" % v for v in range(NV)] + ["lit%d" % v for v in range(NV)]
+              + ["op%d" % k for k in range(NOPS)])
+
+
+def rank_program(g, core, T, topo):
+    r = T.rank_of(core)
+    if r is None:
+        return
+    A = AluOpType
+    F = ActivationFunctionType
+    vec, act, pe, syn = g.vector, g.scalar, g.tensor, g.sync
+    queues = {"g": g, "v": vec, "a": act, "p": pe, "s": syn}
+    seen = {}
+    count = [0]
+
+    def wait(q, *deps):
+        for d in deps:
+            if d is not None and (q, d) not in seen:
+                seen[(q, d)] = True
+                queues[q].wait_ge(T.sem[d[0]], d[1])
+
+    def mark(ins):
+        name = "op%d" % count[0]
+        count[0] += 1
+        ins.then_inc(T.sem[name], 1)
+        return (name, 1)
+
+    later = [d for d in range(NV - 1, r, -1)]
+
+    syn.dma_start(T.lni[0:8, :], T.ln[:]).then_inc(T.sem.d_ln, 16)
+    act.dma_start(T.fri[0:8, :], T.frm[:]).then_inc(T.sem.d_fr, 16)
+    syn.dma_start(T.liti[:], T.lit[:]).then_inc(T.sem.d_li, 16)
+
+    m_one = mark(vec.memset(T.one[:], 1.0))
+    m_q2 = mark(vec.memset(T.qm2[:], 512.0))
+    m_q1 = mark(vec.memset(T.qm1[:], -512.0))
+    m_zf = mark(vec.memset(T.zf[0:8, :], 0.0))
+    m_st = mark(vec.memset(T.stf[0:8, 0:1], 0.0))
+    m_ex = mark(vec.memset(T.exi[0:8, 0:1], 0))
+    m_c16 = mark(vec.memset(T.c16[0:1, :], 16.0))
+    m_neg = mark(vec.memset(T.cneg[0:1, :], -2048.0)) if r == 0 else None
+    m_x = {}
+    for b in ("xm", "xq", "xh", "xl"):
+        m_x[b] = mark(vec.memset(T[b][0:8, :], 0.0))
+    m_ap = mark(vec.memset(T.ap[:], 0.0))
+    m_am = mark(vec.memset(T.am[:], 0.0))
+    m_w = []
+    for v in range(r + 1):
+        m_w.append(mark(vec.memset(T.wl[:] if v == 0 else T["w%d" % (v - 1)][:, S:S + Q], 0.0)))
+
+    imp = {"allow_small_or_imprecise_dtypes": True}
+    wait("g", m_one)
+    c_sele = mark(g.affine_select(T.sele[0:8, 0:4], T.one[0:8, 0:4], [[-2, 4]], A.is_equal, 0.0, 0, 1))
+    wait("g", c_sele)
+    c_selo = mark(g.affine_select(T.selo[0:8, 0:4], T.one[0:8, 0:4], [[-2, 4]], A.is_equal, 0.0, -1, 1))
+    wait("g", c_selo)
+    c_iom = mark(g.iota(T.iom[:, 0:129], [[1, 129]], -1, 0, **imp))
+    wait("g", c_iom, m_q2)
+    c_q2a = mark(g.iota(T.qm2[0:64, 0:16], [[1, 16]], 0, 0, **imp))
+    wait("g", c_q2a)
+    c_q2b = mark(g.iota(T.qm2[64:128, 16:32], [[1, 16]], 0, 0, **imp))
+    wait("g", c_q2b, m_q1)
+    c_q1a = mark(g.iota(T.qm1[0:64, 0:16], [[1, 16]], 0, 0, **imp))
+    wait("g", c_q1a)
+    c_q1b = mark(g.iota(T.qm1[64:128, 16:32], [[1, 16]], 0, 0, **imp))
+    wait("g", c_q1b)
+    c_qrow = mark(g.iota(T.qrow[0:1, :], [[0, 8], [1, 16]], 0, 0, **imp))
+
+    wait("v", ("d_ln", 16), m_zf)
+    o_lnf = mark(vec.tensor_copy(T.lnf[0:8, :], T.lni[0:8, :]))
+    wait("v", ("d_fr", 16), m_ex)
+    o_ex = mark(vec.tensor_tensor(T.exi[0:8, 1:65], T.fri[0:8, :], T.lni[0:8, :], A.add))
+    wait("v", o_lnf, m_st)
+    o_st = mark(vec.tensor_tensor_scan(T.stf[0:8, 1:65], T.lnf[0:8, :], T.zf[0:8, :], 0.0, A.add, A.add))
+    wait("v", o_ex, m_x["xh"])
+    o_xh = mark(vec.tensor_tensor(T.xh[0:8, 64:128], T.fri[0:8, :], T.exi[0:8, 0:64], A.subtract))
+    o_dl = mark(vec.tensor_tensor(T.dlt[0:8, :], T.fri[0:8, :], T.exi[0:8, 0:64], A.subtract))
+    wait("v", o_st)
+    o_sti = mark(vec.tensor_copy(T.sti[0:8, :], T.stf[0:8, 0:64]))
+    wait("v", o_dl, o_xh, m_x["xl"])
+    o_xl = mark(vec.tensor_tensor(T.xl[0:8, 64:128], T.dlt[0:8, :], T.xh[0:8, 64:128], A.subtract))
+    wait("v", o_sti)
+    o_sqi = mark(vec.tensor_scalar(T.sqi[0:8, :], T.sti[0:8, :], 15, None, A.bitwise_and))
+    o_smi = mark(vec.tensor_scalar(T.smi[0:8, :], T.sti[0:8, :], 4, None, A.arith_shift_right))
+    wait("v", o_sqi, m_x["xq"])
+    o_xq = mark(vec.tensor_copy(T.xq[0:8, 64:128], T.sqi[0:8, :]))
+    wait("v", o_smi, m_x["xm"])
+    o_xm = mark(vec.tensor_copy(T.xm[0:8, 64:128], T.smi[0:8, :]))
+    wait("v", ("d_li", 16))
+    o_lb = mark(vec.tensor_copy(T.litb[:], T.liti[:]))
+
+    wait("p", m_c16, c_iom)
+    pe.matmul(T.pout[:, 0:128], T.c16[0:1, :], T.iom[0:1, 1:129], True, False)
+    wait("p", c_sele, c_selo)
+    p_col = {}
+    for ps, x, dep in (("pdh", "xh", o_xh), ("pdl", "xl", o_xl), ("psq", "xq", o_xq), ("psm", "xm", o_xm)):
+        wait("p", dep)
+        pe.matmul(T[ps][:, 0:4], T[x][0:8, 64:192], T.sele[0:8, 0:4], True, False)
+        p_col[ps] = mark(pe.matmul(T[ps][:, 0:4], T[x][0:8, 0:128], T.selo[0:8, 0:4], False, True))
+    wait("p", c_qrow, m_one, m_neg)
+    pe.matmul(T.pout[:, 0:128], T.qrow[0:1, :], T.one[0:1, :], False, False)
+    if r == 0:
+        pe.matmul(T.pout[:, 0:128], T.cneg[0:1, :], T.one[0:1, :], False, False)
+
+    wait("a", p_col["psq"])
+    a_bc = mark(act.activation(T.bcol[:], T.psq[:, 0:4], F.Identity, bias=-0.5))
+    wait("a", a_bc, c_q2a, c_q2b)
+    a_sg = []
+    for b in range(4):
+        a_sg.append(mark(act.activation(T.sgn[:, 32 * b:32 * b + 32], T.qm2[:], F.Sign, bias=T.bcol[:, b:b + 1], scale=-1.0)))
+    wait("a", m_am)
+    a_am = []
+    for b in range(4):
+        wait("a", a_sg[b])
+        a_am.append(mark(act.activation(T.am[:, 160 * b:160 * b + 32], T.sgn[:, 32 * b:32 * b + 32], F.Relu)))
+    v_bh, v_bl, v_ap = [], [], []
+    wait("v", c_iom, p_col["pdh"], p_col["psm"])
+    for b in range(4):
+        v_bh.append(mark(vec.tensor_scalar(T.bh[:, BW * b:BW * b + 129], T.iom[:, 0:129], T.psm[:, b:b + 1], T.pdh[:, b:b + 1],
+                                           A.is_ge, A.mult)))
+        wait("v", p_col["pdl"])
+        v_bl.append(mark(vec.tensor_scalar(T.bl[:, BW * b:BW * b + 129], T.iom[:, 0:129], T.psm[:, b:b + 1], T.pdl[:, b:b + 1],
+                                           A.is_ge, A.mult)))
+        wait("v", a_bc, c_q1a, c_q1b, m_ap)
+        v_ap.append(mark(vec.tensor_scalar(T.ap[:, 160 * b:160 * b + 32], T.qm1[:], T.bcol[:, b:b + 1], None, A.is_ge)))
+    last = None
+    for b in range(4):
+        lp, lm = T.ap[:, 128 * b:128 * b + 128], T.am[:, 128 * b:128 * b + 128]
+        now_h, now_l = T.bh[:, BW * b + 1:BW * b + 129], T.bl[:, BW * b + 1:BW * b + 129]
+        old_h, old_l = T.bh[:, BW * b:BW * b + 128], T.bl[:, BW * b:BW * b + 128]
+        wait("p", v_bh[b], v_bl[b], v_ap[b])
+        pe.matmul(T.pout[:, 0:128], lp, now_h, False, False)
+        pe.matmul(T.pout[:, 0:128], lp, now_l, False, False)
+        wait("p", a_am[b])
+        pe.matmul(T.pout[:, 0:128], lm, old_h, False, False)
+        last = pe.matmul(T.pout[:, 0:128], lm, old_l, False, b == 3)
+    p_out = mark(last)
+    own = T["ls%d" % r]
+    wait("v", p_out)
+    o_ls = mark(vec.tensor_copy(own[:], T.pout[:, 0:128]))
+
+    def send(src, dst, dests, sem, local):
+        mask = topo.mask(core, T.cores[dests[0]])
+        ids = []
+        for d in dests:
+            rid, pid, _se = topo.addr(T.cores[d])
+            ids.append(DstId(rid=rid, pnc=pid))
+        g.remote_dma_fused([RemoteDMATransfer(dst_ids=ids, dma_engine_mask=mask, remote_sem=T.sem[sem],
+                                              srcs=[src], dsts=[dst] * len(dests))], local_sem=T.sem[local])
+        return len(topo.engines(core, T.cores[dests[0]]))
+
+    if later:
+        wait("g", o_lb)
+        nk = send(T.litb[:], T.lland[r], later, "arrk%d" % r, "loc_k")
+        n = len(later)
+        if r < 2:
+            calls = [later[:1], later[1:]]
+        else:
+            k = min(r, n - 1)
+            calls = [later[n - k:] + later[:n - k]]
+        wait("g", o_ls)
+        nl = 0
+        for c in calls:
+            nl += send(own[:], own[:], c, "arrl%d" % r, "loc_l")
+
+    for v in range(r + 1):
+        dst = T.wl[0:128:16, :] if v == 0 else T["w%d" % (v - 1)][0:128:16, S:S + Q]
+        wait("s", m_w[v])
+        if v == r:
+            wait("s", o_lb)
+            syn.dma_start(dst, T.litb[:]).then_inc(T.sem["lit%d" % v], 16)
+        else:
+            wait("s", ("arrk%d" % v, len(topo.engines(T.cores[v], core))))
+            syn.dma_start(dst, T.lland[v]).then_inc(T.sem["lit%d" % v], 16)
+
+    prev = []
+    for v in range(r + 1):
+        win = T.wl[:] if v == 0 else T["w%d" % (v - 1)][:]
+        lst = T["ls%d" % v]
+        out = T.yo if v == r else T["w%d" % v]
+        got = o_ls if v == r else ("arrl%d" % v, len(topo.engines(T.cores[v], core)))
+        for q in ("v", "a"):
+            wait(q, ("lit%d" % v, 16), got, *prev)
+        prev = [mark(vec.tensor_copy(out[:, 0:HALF], win.indirect(lst[:, 0:64]))),
+                mark(act.activation(out[:, HALF:S], win.indirect(lst[:, 64:128]), F.Copy))]
+    wait("s", prev[0])
+    syn.dma_start(T.y[:, 0:HALF], T.yo[0:128:16, 0:HALF]).then_inc(T.sem.d_y0, 16)
+    wait("a", prev[1])
+    act.dma_start(T.y[:, HALF:S], T.yo[0:128:16, HALF:S]).then_inc(T.sem.d_y1, 16)
+    if later:
+        g.wait_ge(T.sem.loc_k, nk)
+        g.wait_ge(T.sem.loc_l, nl)
+    syn.wait_ge(T.sem.d_y0, 16)
+    act.wait_ge(T.sem.d_y1, 16)

@@ -6,6 +6,14 @@ S = 2048
 Q = 512
 HALF = S // 2
 BW = 136
+IDN = S + Q
+BIG = float(3 * 2 ** 26)
+
+JOIN = {
+    2: (4, 5, 0, 64, "ca", "arrc0", [[7], [6, 5]]),
+    3: (4, 5, 64, 64, "cb", "arrc1", [[7], [6, 5]]),
+    1: (6, 7, 0, 128, "cf", "arrc2", [[7]]),
+}
 
 SCRATCH = {
     "lni": ("sbuf", [128, 64], "int32"),
@@ -15,48 +23,66 @@ SCRATCH = {
     "lnf": ("sbuf", [128, 64], "float32"),
     "zf": ("sbuf", [128, 64], "float32"),
     "stf": ("sbuf", [128, 72], "float32"),
-    "sti": ("sbuf", [128, 64], "int32"),
-    "smi": ("sbuf", [128, 64], "int32"),
-    "sqi": ("sbuf", [128, 64], "int32"),
     "exi": ("sbuf", [128, 72], "int32"),
     "dlt": ("sbuf", [128, 64], "float32"),
-    "xm": ("sbuf", [128, 192], "bfloat16"),
-    "xq": ("sbuf", [128, 192], "bfloat16"),
-    "xh": ("sbuf", [128, 192], "bfloat16"),
-    "xl": ("sbuf", [128, 192], "bfloat16"),
+    "xx": ("sbuf", [128, 576], "bfloat16"),
     "iom": ("sbuf", [128, 136], "bfloat16"),
     "qm1": ("sbuf", [128, 32], "bfloat16"),
     "qm2": ("sbuf", [128, 32], "bfloat16"),
-    "one": ("sbuf", [128, 128], "bfloat16"),
+    "one": ("sbuf", [128, 144], "bfloat16"),
     "sele": ("sbuf", [128, 8], "bfloat16"),
     "selo": ("sbuf", [128, 8], "bfloat16"),
-    "c16": ("sbuf", [128, 128], "bfloat16"),
     "cneg": ("sbuf", [128, 128], "bfloat16"),
     "qrow": ("sbuf", [128, 128], "bfloat16"),
-    "bcol": ("sbuf", [128, 4], "float32"),
-    "sgn": ("sbuf", [128, 128], "bfloat16"),
+    "bcp": ("sbuf", [128, 4], "float32"),
+    "bcn": ("sbuf", [128, 4], "float32"),
     "ap": ("sbuf", [128, 512], "bfloat16"),
     "am": ("sbuf", [128, 512], "bfloat16"),
     "bh": ("sbuf", [128, 4 * BW], "bfloat16"),
     "bl": ("sbuf", [128, 4 * BW], "bfloat16"),
     "wl": ("sbuf", [128, Q], "bfloat16"),
+    "w0": ("sbuf", [128, S + Q], "bfloat16"),
+    "w1": ("sbuf", [128, S + Q], "bfloat16"),
+    "w2": ("sbuf", [128, S + Q], "bfloat16"),
+    "w3": ("sbuf", [128, S + 2 * Q], "bfloat16"),
+    "w5": ("sbuf", [128, S + 2 * Q], "bfloat16"),
     "yo": ("sbuf", [128, S], "float32"),
     "lland": ("dram", [NV, 128, 32], "bfloat16"),
+    "pci": ("sbuf", [128, 8], "int32"),
+    "p15": ("sbuf", [128, 8], "int32"),
+    "h5": ("sbuf", [128, 4], "float32"),
+    "h80": ("sbuf", [128, 4], "float32"),
+    "pm0": ("sbuf", [128, 4], "float32"),
+    "pm1": ("sbuf", [128, 4], "float32"),
+    "lo": ("sbuf", [128, 160], "bfloat16"),
+    "hib": ("sbuf", [128, 160], "bfloat16"),
+    "hi": ("sbuf", [128, 160], "bfloat16"),
+    "hix": ("sbuf", [128, 32], "bfloat16"),
+    "d15": ("sbuf", [128, 144], "bfloat16"),
+    "d14": ("sbuf", [128, 144], "bfloat16"),
+    "e15": ("sbuf", [128, 144], "bfloat16"),
+    "e14": ("sbuf", [128, 144], "bfloat16"),
+    "ee": ("sbuf", [128, 144], "bfloat16"),
+    "idw": ("sbuf", [128, IDN], "bfloat16"),
+    "cw": ("sbuf", [128, S + Q], "bfloat16"),
+    "cr": ("sbuf", [128, S], "bfloat16"),
+    "ca": ("sbuf", [128, 64], "uint16"),
+    "cb": ("sbuf", [128, 64], "uint16"),
+    "cf": ("sbuf", [128, 128], "uint16"),
     "psm": ("psum", [128, 512], "float32"),
     "psq": ("psum", [128, 512], "float32"),
     "pdh": ("psum", [128, 512], "float32"),
     "pdl": ("psum", [128, 512], "float32"),
     "pout": ("psum", [128, 512], "float32"),
+    "pjn": ("psum", [128, 512], "float32"),
 }
 for _v in range(NV):
     SCRATCH["ls%d" % _v] = ("sbuf", [128, 128], "uint16")
-for _v in range(NV - 1):
-    SCRATCH["w%d" % _v] = ("sbuf", [128, S + Q], "bfloat16")
 
-NOPS = 100
-SEMAPHORES = (["d_ln", "d_fr", "d_li", "d_y0", "d_y1", "loc_k", "loc_l"]
-              + ["arrk%d" % v for v in range(NV)] + ["arrl%d" % v for v in range(NV)] + ["lit%d" % v for v in range(NV)]
-              + ["op%d" % k for k in range(NOPS)])
+NOPS = 112
+SEMAPHORES = (["d_ln", "d_fr", "d_li", "d_y0", "d_y1", "d_id", "d_cw", "loc", "arrc0", "arrc1", "arrc2"]
+              + ["arrk%d" % v for v in range(NV - 1)] + ["arrl%d" % v for v in range(NV)]
+              + ["lit%d" % v for v in range(NV)] + ["op%d" % k for k in range(NOPS)])
 
 
 def rank_program(g, core, T, topo):
@@ -68,184 +94,301 @@ def rank_program(g, core, T, topo):
     vec, act, pe, syn = g.vector, g.scalar, g.tensor, g.sync
     queues = {"g": g, "v": vec, "a": act, "p": pe, "s": syn}
     seen = {}
-    count = [0]
+    waited = {}
+    marks = []
+    helper = r in JOIN
 
     def wait(q, *deps):
         for d in deps:
             if d is not None and (q, d) not in seen:
                 seen[(q, d)] = True
+                waited[d[0]] = True
                 queues[q].wait_ge(T.sem[d[0]], d[1])
 
     def mark(ins):
-        name = "op%d" % count[0]
-        count[0] += 1
+        name = "op%d" % len(marks)
+        marks.append(name)
         ins.then_inc(T.sem[name], 1)
         return (name, 1)
 
-    later = [d for d in range(NV - 1, r, -1)]
+    def arrived(name, src):
+        return (name, len(topo.engines(T.cores[src], core)))
 
-    syn.dma_start(T.lni[0:8, :], T.ln[:]).then_inc(T.sem.d_ln, 16)
-    act.dma_start(T.fri[0:8, :], T.frm[:]).then_inc(T.sem.d_fr, 16)
-    syn.dma_start(T.liti[:], T.lit[:]).then_inc(T.sem.d_li, 16)
+    if r <= 4:
+        stages = [[v] for v in range(r + 1)]
+    else:
+        stages = [[0], [1], [2], [3], [4, 5]] + ([[6]] if r == 6 else [[6, 7]] if r == 7 else [])
+    wins = [T.wl] + [T["w%d" % st[-1]] for st in stages[:-1]]
+    base = [0] + [S] * (len(stages) - 1)
+
+    if r == 0:
+        syn.dma_start(T.liti[:], T.lit[:]).then_inc(T.sem.d_li, 16)
+        act.dma_start(T.lni[0:8, :], T.ln[:]).then_inc(T.sem.d_ln, 16)
+        syn.dma_start(T.fri[0:8, :], T.frm[:]).then_inc(T.sem.d_fr, 16)
+    else:
+        syn.dma_start(T.lni[0:8, :], T.ln[:]).then_inc(T.sem.d_ln, 16)
+        act.dma_start(T.fri[0:8, :], T.frm[:]).then_inc(T.sem.d_fr, 16)
+        syn.dma_start(T.liti[:], T.lit[:]).then_inc(T.sem.d_li, 16)
+
+    m_w = {}
+
+    def zero_window(k):
+        m_w[k] = mark(vec.memset(wins[k][:, base[k]:base[k] + Q * len(stages[k])], 0.0))
 
     m_one = mark(vec.memset(T.one[:], 1.0))
-    m_q2 = mark(vec.memset(T.qm2[:], 512.0))
+    if helper:
+        m_id0 = mark(vec.memset(T.idw[:, 0:IDN // 2], 0.0))
+    else:
+        m_ap = mark(vec.memset(T.ap[:], 0.0))
     m_q1 = mark(vec.memset(T.qm1[:], -512.0))
+    m_q2 = mark(vec.memset(T.qm2[:], 512.0))
     m_zf = mark(vec.memset(T.zf[0:8, :], 0.0))
-    m_st = mark(vec.memset(T.stf[0:8, 0:1], 0.0))
+    m_st = mark(vec.memset(T.stf[0:8, 0:1], -7.5))
     m_ex = mark(vec.memset(T.exi[0:8, 0:1], 0))
-    m_c16 = mark(vec.memset(T.c16[0:1, :], 16.0))
     m_neg = mark(vec.memset(T.cneg[0:1, :], -2048.0)) if r == 0 else None
-    m_x = {}
-    for b in ("xm", "xq", "xh", "xl"):
-        m_x[b] = mark(vec.memset(T[b][0:8, :], 0.0))
-    m_ap = mark(vec.memset(T.ap[:], 0.0))
-    m_am = mark(vec.memset(T.am[:], 0.0))
-    m_w = []
-    for v in range(r + 1):
-        m_w.append(mark(vec.memset(T.wl[:] if v == 0 else T["w%d" % (v - 1)][:, S:S + Q], 0.0)))
+    m_xx = mark(vec.memset(T.xx[0:8, :], 0.0))
+    if helper:
+        m_ap = mark(vec.memset(T.ap[:], 0.0))
+        m_am = mark(vec.memset(T.am[:], 0.0))
+    if r > 0:
+        zero_window(0)
+        zero_window(1)
+    if helper:
+        wait("a", m_id0)
+        m_id1 = mark(act.activation(T.idw[:, IDN // 2:IDN], T.idw[:, 0:IDN // 2], F.Sigmoid, bias=-200.0))
+    else:
+        wait("a", m_ap)
+        m_am = mark(act.activation(T.am[:], T.ap[:], F.Sigmoid, bias=-200.0))
 
     imp = {"allow_small_or_imprecise_dtypes": True}
-    wait("g", m_one)
-    c_sele = mark(g.affine_select(T.sele[0:8, 0:4], T.one[0:8, 0:4], [[-2, 4]], A.is_equal, 0.0, 0, 1))
-    wait("g", c_sele)
-    c_selo = mark(g.affine_select(T.selo[0:8, 0:4], T.one[0:8, 0:4], [[-2, 4]], A.is_equal, 0.0, -1, 1))
-    wait("g", c_selo)
-    c_iom = mark(g.iota(T.iom[:, 0:129], [[1, 129]], -1, 0, **imp))
-    wait("g", c_iom, m_q2)
-    c_q2a = mark(g.iota(T.qm2[0:64, 0:16], [[1, 16]], 0, 0, **imp))
-    wait("g", c_q2a)
-    c_q2b = mark(g.iota(T.qm2[64:128, 16:32], [[1, 16]], 0, 0, **imp))
-    wait("g", c_q2b, m_q1)
-    c_q1a = mark(g.iota(T.qm1[0:64, 0:16], [[1, 16]], 0, 0, **imp))
-    wait("g", c_q1a)
-    c_q1b = mark(g.iota(T.qm1[64:128, 16:32], [[1, 16]], 0, 0, **imp))
-    wait("g", c_q1b)
-    c_qrow = mark(g.iota(T.qrow[0:1, :], [[0, 8], [1, 16]], 0, 0, **imp))
+    chain = [None]
 
-    wait("v", ("d_ln", 16), m_zf)
+    def gp(ins):
+        chain[0] = mark(ins)
+        return chain[0]
+
+    wait("g", m_one)
+    c_sele = gp(g.affine_select(T.sele[0:8, 0:4], T.one[0:8, 0:4], [[-2, 4]], A.is_equal, 0.0, 0, 1))
+    wait("g", chain[0])
+    c_selo = gp(g.affine_select(T.selo[0:8, 0:4], T.one[0:8, 0:4], [[-2, 4]], A.is_equal, 0.0, -1, 1))
+    wait("g", chain[0])
+    c_iom = gp(g.iota(T.iom[:, 0:129], [[16, 129]], -16, 0, **imp))
+    wait("g", chain[0], m_q1)
+    c_q1a = gp(g.iota(T.qm1[0:64, 0:16], [[1, 16]], -7, 0, **imp))
+    wait("g", chain[0])
+    c_q1b = gp(g.iota(T.qm1[64:128, 16:32], [[1, 16]], -7, 0, **imp))
+    wait("g", chain[0], m_q2)
+    c_q2a = gp(g.iota(T.qm2[0:64, 0:16], [[1, 16]], -7, 0, **imp))
+    wait("g", chain[0])
+    c_q2b = gp(g.iota(T.qm2[64:128, 16:32], [[1, 16]], -7, 0, **imp))
+    wait("g", chain[0])
+    c_qrow = gp(g.iota(T.qrow[0:1, :], [[0, 8], [1, 16]], 0, 0, **imp))
+    if helper:
+        wait("g", chain[0])
+        c_pci = gp(g.iota(T.pci[:, 0:1], [[0, 1]], 0, 1))
+        wait("g", chain[0])
+        c_hib = gp(g.iota(T.hib[:], [[1, 5], [0, 32]], 0, 0, **imp))
+        wait("g", chain[0])
+        c_lo = gp(g.iota(T.lo[:], [[0, 5], [1, 32]], 0, 0, **imp))
+
+    def xs(k):
+        return T.xx[0:8, 64 + 128 * k:128 + 128 * k]
+
+    if r == 0:
+        wait("v", ("d_li", 16))
+        o_lb = mark(vec.tensor_copy(T.litb[:], T.liti[:]))
+    wait("v", ("d_ln", 16))
     o_lnf = mark(vec.tensor_copy(T.lnf[0:8, :], T.lni[0:8, :]))
     wait("v", ("d_fr", 16), m_ex)
     o_ex = mark(vec.tensor_tensor(T.exi[0:8, 1:65], T.fri[0:8, :], T.lni[0:8, :], A.add))
-    wait("v", o_lnf, m_st)
-    o_st = mark(vec.tensor_tensor_scan(T.stf[0:8, 1:65], T.lnf[0:8, :], T.zf[0:8, :], 0.0, A.add, A.add))
-    wait("v", o_ex, m_x["xh"])
-    o_xh = mark(vec.tensor_tensor(T.xh[0:8, 64:128], T.fri[0:8, :], T.exi[0:8, 0:64], A.subtract))
-    o_dl = mark(vec.tensor_tensor(T.dlt[0:8, :], T.fri[0:8, :], T.exi[0:8, 0:64], A.subtract))
+    wait("v", o_lnf, m_st, m_zf)
+    o_st = mark(vec.tensor_tensor_scan(T.stf[0:8, 1:65], T.lnf[0:8, :], T.zf[0:8, :], -7.5, A.add, A.add))
+    wait("v", o_ex, m_xx)
+    o_xh = mark(vec.tensor_tensor(xs(1), T.fri[0:8, :], T.exi[0:8, 0:64], A.subtract))
     wait("v", o_st)
-    o_sti = mark(vec.tensor_copy(T.sti[0:8, :], T.stf[0:8, 0:64]))
-    wait("v", o_dl, o_xh, m_x["xl"])
-    o_xl = mark(vec.tensor_tensor(T.xl[0:8, 64:128], T.dlt[0:8, :], T.xh[0:8, 64:128], A.subtract))
-    wait("v", o_sti)
-    o_sqi = mark(vec.tensor_scalar(T.sqi[0:8, :], T.sti[0:8, :], 15, None, A.bitwise_and))
-    o_smi = mark(vec.tensor_scalar(T.smi[0:8, :], T.sti[0:8, :], 4, None, A.arith_shift_right))
-    wait("v", o_sqi, m_x["xq"])
-    o_xq = mark(vec.tensor_copy(T.xq[0:8, 64:128], T.sqi[0:8, :]))
-    wait("v", o_smi, m_x["xm"])
-    o_xm = mark(vec.tensor_copy(T.xm[0:8, 64:128], T.smi[0:8, :]))
-    wait("v", ("d_li", 16))
-    o_lb = mark(vec.tensor_copy(T.litb[:], T.liti[:]))
+    o_xm = mark(vec.tensor_scalar(xs(0), T.stf[0:8, 0:64], BIG, -BIG, A.add, A.add))
+    o_dl = mark(vec.tensor_tensor(T.dlt[0:8, :], T.fri[0:8, :], T.exi[0:8, 0:64], A.subtract))
+    wait("v", o_xm)
+    o_xq = mark(vec.tensor_tensor(xs(2), xs(0), T.stf[0:8, 0:64], A.subtract))
+    wait("v", o_dl, o_xh)
+    o_xl = mark(vec.tensor_tensor(xs(3), T.dlt[0:8, :], xs(1), A.subtract))
+    if r > 0:
+        wait("v", ("d_li", 16))
+        o_lb = mark(vec.tensor_copy(T.litb[:], T.liti[:]))
 
-    wait("p", m_c16, c_iom)
-    pe.matmul(T.pout[:, 0:128], T.c16[0:1, :], T.iom[0:1, 1:129], True, False)
-    wait("p", c_sele, c_selo)
+    wait("p", c_iom, m_one)
+    pe.matmul(T.pout[:, 0:128], T.one[0:1, 0:128], T.iom[0:1, 1:129], True, False)
+    wait("p", c_sele, c_selo, m_xx)
     p_col = {}
-    for ps, x, dep in (("pdh", "xh", o_xh), ("pdl", "xl", o_xl), ("psq", "xq", o_xq), ("psm", "xm", o_xm)):
+    for ps, k, dep in (("pdh", 1, o_xh), ("psm", 0, o_xm), ("psq", 2, o_xq), ("pdl", 3, o_xl)):
         wait("p", dep)
-        pe.matmul(T[ps][:, 0:4], T[x][0:8, 64:192], T.sele[0:8, 0:4], True, False)
-        p_col[ps] = mark(pe.matmul(T[ps][:, 0:4], T[x][0:8, 0:128], T.selo[0:8, 0:4], False, True))
-    wait("p", c_qrow, m_one, m_neg)
-    pe.matmul(T.pout[:, 0:128], T.qrow[0:1, :], T.one[0:1, :], False, False)
+        pe.matmul(T[ps][:, 0:4], T.xx[0:8, 64 + 128 * k:192 + 128 * k], T.sele[0:8, 0:4], True, False)
+        p_col[ps] = mark(pe.matmul(T[ps][:, 0:4], T.xx[0:8, 128 * k:128 + 128 * k], T.selo[0:8, 0:4], False, True))
+    wait("p", c_qrow, m_neg)
+    pe.matmul(T.pout[:, 0:128], T.qrow[0:1, :], T.one[0:1, 0:128], False, False)
     if r == 0:
-        pe.matmul(T.pout[:, 0:128], T.cneg[0:1, :], T.one[0:1, :], False, False)
+        pe.matmul(T.pout[:, 0:128], T.cneg[0:1, :], T.one[0:1, 0:128], False, False)
 
     wait("a", p_col["psq"])
-    a_bc = mark(act.activation(T.bcol[:], T.psq[:, 0:4], F.Identity, bias=-0.5))
-    wait("a", a_bc, c_q2a, c_q2b)
-    a_sg = []
+    a_bp = mark(act.activation(T.bcp[:], T.psq[:, 0:4], F.Identity, scale=256.0))
+    a_bn = mark(act.activation(T.bcn[:], T.psq[:, 0:4], F.Identity, scale=-256.0))
+    wait("a", m_ap, m_am, c_q1a, c_q1b, c_q2a, c_q2b, a_bp, a_bn)
+    a_lf = []
     for b in range(4):
-        a_sg.append(mark(act.activation(T.sgn[:, 32 * b:32 * b + 32], T.qm2[:], F.Sign, bias=T.bcol[:, b:b + 1], scale=-1.0)))
-    wait("a", m_am)
-    a_am = []
-    for b in range(4):
-        wait("a", a_sg[b])
-        a_am.append(mark(act.activation(T.am[:, 160 * b:160 * b + 32], T.sgn[:, 32 * b:32 * b + 32], F.Relu)))
-    v_bh, v_bl, v_ap = [], [], []
+        la = mark(act.activation(T.ap[:, 160 * b:160 * b + 32], T.qm1[:], F.Sigmoid, bias=T.bcp[:, b:b + 1], scale=256.0))
+        lb = mark(act.activation(T.am[:, 160 * b:160 * b + 32], T.qm2[:], F.Sigmoid, bias=T.bcn[:, b:b + 1], scale=-256.0))
+        a_lf.append((la, lb))
+    v_b = []
     wait("v", c_iom, p_col["pdh"], p_col["psm"])
     for b in range(4):
-        v_bh.append(mark(vec.tensor_scalar(T.bh[:, BW * b:BW * b + 129], T.iom[:, 0:129], T.psm[:, b:b + 1], T.pdh[:, b:b + 1],
-                                           A.is_ge, A.mult)))
+        vh = mark(vec.tensor_scalar(T.bh[:, BW * b:BW * b + 129], T.iom[:, 0:129], T.psm[:, b:b + 1], T.pdh[:, b:b + 1],
+                                    A.is_ge, A.mult))
         wait("v", p_col["pdl"])
-        v_bl.append(mark(vec.tensor_scalar(T.bl[:, BW * b:BW * b + 129], T.iom[:, 0:129], T.psm[:, b:b + 1], T.pdl[:, b:b + 1],
-                                           A.is_ge, A.mult)))
-        wait("v", a_bc, c_q1a, c_q1b, m_ap)
-        v_ap.append(mark(vec.tensor_scalar(T.ap[:, 160 * b:160 * b + 32], T.qm1[:], T.bcol[:, b:b + 1], None, A.is_ge)))
+        vl = mark(vec.tensor_scalar(T.bl[:, BW * b:BW * b + 129], T.iom[:, 0:129], T.psm[:, b:b + 1], T.pdl[:, b:b + 1],
+                                    A.is_ge, A.mult))
+        v_b.append((vh, vl))
     last = None
     for b in range(4):
         lp, lm = T.ap[:, 128 * b:128 * b + 128], T.am[:, 128 * b:128 * b + 128]
         now_h, now_l = T.bh[:, BW * b + 1:BW * b + 129], T.bl[:, BW * b + 1:BW * b + 129]
         old_h, old_l = T.bh[:, BW * b:BW * b + 128], T.bl[:, BW * b:BW * b + 128]
-        wait("p", v_bh[b], v_bl[b], v_ap[b])
+        wait("p", v_b[b][0], v_b[b][1], a_lf[b][0])
         pe.matmul(T.pout[:, 0:128], lp, now_h, False, False)
         pe.matmul(T.pout[:, 0:128], lp, now_l, False, False)
-        wait("p", a_am[b])
+        wait("p", a_lf[b][1])
         pe.matmul(T.pout[:, 0:128], lm, old_h, False, False)
         last = pe.matmul(T.pout[:, 0:128], lm, old_l, False, b == 3)
     p_out = mark(last)
+    if helper:
+        wait("v", c_pci)
+        o_p15 = mark(vec.tensor_scalar(T.p15[:, 0:1], T.pci[:, 0:1], 15, None, A.bitwise_and))
+        wait("v", o_p15)
+        o_h5 = mark(vec.tensor_scalar(T.h5[:, 0:1], T.p15[:, 0:1], 5.0, None, A.mult))
+        o_h80 = mark(vec.tensor_scalar(T.h80[:, 0:1], T.p15[:, 0:1], 80.0, None, A.add))
     own = T["ls%d" % r]
     wait("v", p_out)
     o_ls = mark(vec.tensor_copy(own[:], T.pout[:, 0:128]))
 
-    def send(src, dst, dests, sem, local):
+    sent = [0]
+
+    def send(src, dst, dests, sem):
         mask = topo.mask(core, T.cores[dests[0]])
         ids = []
         for d in dests:
             rid, pid, _se = topo.addr(T.cores[d])
             ids.append(DstId(rid=rid, pnc=pid))
         g.remote_dma_fused([RemoteDMATransfer(dst_ids=ids, dma_engine_mask=mask, remote_sem=T.sem[sem],
-                                              srcs=[src], dsts=[dst] * len(dests))], local_sem=T.sem[local])
-        return len(topo.engines(core, T.cores[dests[0]]))
+                                              srcs=[src], dsts=[dst] * len(dests))], local_sem=T.sem.loc)
+        sent[0] += len(topo.engines(core, T.cores[dests[0]]))
 
-    if later:
+    far = [d for d in range(NV - 1, r, -1) if d >= 4]
+    near = [d for d in range(3, r, -1)]
+    if far:
         wait("g", o_lb)
-        nk = send(T.litb[:], T.lland[r], later, "arrk%d" % r, "loc_k")
-        n = len(later)
-        if r < 2:
-            calls = [later[:1], later[1:]]
-        else:
-            k = min(r, n - 1)
-            calls = [later[n - k:] + later[:n - k]]
-        wait("g", o_ls)
-        nl = 0
-        for c in calls:
-            nl += send(own[:], own[:], c, "arrl%d" % r, "loc_l")
+        send(T.litb[:], T.lland[r], far, "arrk%d" % r)
+    if helper:
+        wait("g", chain[0])
+        c_d15 = gp(g.affine_select(T.d15[:], T.one[:], [[1, 144]], A.is_equal, 0.0, -15, -1))
+        wait("g", chain[0])
+        c_d14 = gp(g.affine_select(T.d14[:], T.one[:], [[1, 144]], A.is_equal, 0.0, -14, -1))
+    wait("g", o_ls)
+    if r <= 3:
+        for c in ([[7], [6], [5, 4]] if r == 0 else [[7, 6], [5, 4]]):
+            send(own[:], own[:], c, "arrl%d" % r)
+    else:
+        send(own[:], own[:], [h for h in JOIN if r in JOIN[h][0:2]], "arrl%d" % r)
+    if near:
+        send(T.litb[:], T.lland[r], near, "arrk%d" % r)
+        send(own[:], own[:], near, "arrl%d" % r)
 
-    for v in range(r + 1):
-        dst = T.wl[0:128:16, :] if v == 0 else T["w%d" % (v - 1)][0:128:16, S:S + Q]
-        wait("s", m_w[v])
-        if v == r:
-            wait("s", o_lb)
-            syn.dma_start(dst, T.litb[:]).then_inc(T.sem["lit%d" % v], 16)
-        else:
-            wait("s", ("arrk%d" % v, len(topo.engines(T.cores[v], core))))
-            syn.dma_start(dst, T.lland[v]).then_inc(T.sem["lit%d" % v], 16)
+    if helper:
+        wait("v", o_p15)
+        o_pm0 = mark(vec.tensor_scalar(T.pm0[:, 0:1], T.p15[:, 0:1], 0.0, None, A.is_equal))
+        o_pm1 = mark(vec.tensor_scalar(T.pm1[:, 0:1], T.p15[:, 0:1], 1.0, 32.0, A.is_equal, A.mult))
+        m_cw = mark(vec.memset(T.cw[:, S:S + Q], 0.0))
+    for k in range(len(stages)):
+        if k not in m_w:
+            zero_window(k)
+    if helper:
+        wait("v", c_d15, c_d14, o_pm0, o_pm1)
+        o_e15 = mark(vec.tensor_scalar(T.e15[:], T.d15[:], T.pm0[:, 0:1], None, A.mult))
+        o_e14 = mark(vec.tensor_scalar(T.e14[:], T.d14[:], T.pm1[:, 0:1], None, A.mult))
+        wait("v", o_e15, o_e14)
+        o_ee = mark(vec.tensor_tensor(T.ee[:], T.e15[:], T.e14[:], A.add))
+        wait("a", c_hib, o_h5)
+        a_hi = mark(act.activation(T.hi[:], T.hib[:], F.Identity, bias=T.h5[:, 0:1]))
+        wait("a", o_h80, m_one)
+        a_hix = mark(act.activation(T.hix[:], T.one[:, 0:32], F.Identity, scale=T.h80[:, 0:1]))
+        wait("s", m_id0, m_id1, c_lo)
+        syn.dma_start(T.idw[0:128:16, :], T.lo[:]).then_inc(T.sem.d_id, 16)
+        wait("s", a_hi)
+        syn.dma_start(T.idw[1:128:16, :], T.hi[:]).then_inc(T.sem.d_id, 16)
+        wait("s", m_cw)
+        syn.dma_start(T.cw[0:128:16, S:S + Q], T.lo[:, 0:32]).then_inc(T.sem.d_cw, 16)
+        wait("s", a_hix)
+        syn.dma_start(T.cw[1:128:16, S:S + Q], T.hix[:]).then_inc(T.sem.d_cw, 16)
+
+    for k in range(len(stages)):
+        for n, v in enumerate(stages[k]):
+            at = base[k] + Q * n
+            dst = wins[k][0:128:16, at:at + Q]
+            wait("s", m_w[k])
+            if v == r:
+                wait("s", o_lb)
+                syn.dma_start(dst, T.litb[:]).then_inc(T.sem["lit%d" % v], 16)
+            else:
+                wait("s", arrived("arrk%d" % v, v))
+                syn.dma_start(dst, T.lland[v]).then_inc(T.sem["lit%d" % v], 16)
+
+    if helper:
+        v0, v1, c0, nc, buf, sem, calls = JOIN[r]
+        l0, l1 = T["ls%d" % v0], T["ls%d" % v1]
+        half = nc // 2
+        for q in ("v", "a"):
+            wait(q, ("d_id", 32), arrived("arrl%d" % v0, v0))
+        i_v = mark(vec.tensor_copy(T.cw[:, 0:HALF], T.idw[:].indirect(l0[:, 0:64])))
+        i_a = mark(act.activation(T.cw[:, HALF:S], T.idw[:].indirect(l0[:, 64:128]), F.Copy))
+        for q in ("v", "a"):
+            wait(q, i_v, i_a, ("d_cw", 32), arrived("arrl%d" % v1, v1))
+        j_v = mark(vec.tensor_copy(T.cr[:, 0:16 * half], T.cw[:].indirect(l1[:, c0:c0 + half])))
+        j_a = mark(act.activation(T.cr[:, 16 * half:16 * nc], T.cw[:].indirect(l1[:, c0 + half:c0 + nc]), F.Copy))
+        wait("p", o_ee, j_v, j_a)
+        for q in range(16):
+            last = pe.matmul(T.pjn[:, 0:nc], T.ee[:, 15 - q:143 - q], T.cr[:, q:16 * nc:16], q == 0, q == 15)
+        p_jn = mark(last)
+        wait("v", p_jn)
+        o_jn = mark(vec.tensor_copy(T[buf][:], T.pjn[:, 0:nc]))
+        wait("g", o_jn)
+        for c in calls:
+            send(T[buf][:], T[buf][:], c, sem)
 
     prev = []
-    for v in range(r + 1):
-        win = T.wl[:] if v == 0 else T["w%d" % (v - 1)][:]
-        lst = T["ls%d" % v]
-        out = T.yo if v == r else T["w%d" % v]
-        got = o_ls if v == r else ("arrl%d" % v, len(topo.engines(T.cores[v], core)))
-        for q in ("v", "a"):
-            wait(q, ("lit%d" % v, 16), got, *prev)
-        prev = [mark(vec.tensor_copy(out[:, 0:HALF], win.indirect(lst[:, 0:64]))),
-                mark(act.activation(out[:, HALF:S], win.indirect(lst[:, 64:128]), F.Copy))]
+    for k, st in enumerate(stages):
+        v = st[-1]
+        win = wins[k][:, 0:base[k] + Q * len(st)]
+        out = T.yo if k == len(stages) - 1 else wins[k + 1]
+        if len(st) == 1:
+            lst = T["ls%d" % v]
+            lists = (lst[:, 0:64], lst[:, 64:128])
+            got = [o_ls if v == r else arrived("arrl%d" % v, v)] * 2
+        elif v == 5:
+            lists = (T.ca[:], T.cb[:])
+            got = [arrived("arrc0", 2), arrived("arrc1", 3)]
+        else:
+            lists = (T.cf[:, 0:64], T.cf[:, 64:128])
+            got = [arrived("arrc2", 1)] * 2
+        lits = [("lit%d" % x, 16) for x in st]
+        wait("v", *lits, got[0], *prev)
+        wait("a", *lits, got[1], *prev)
+        prev = [mark(vec.tensor_copy(out[:, 0:HALF], win.indirect(lists[0]))),
+                mark(act.activation(out[:, HALF:S], win.indirect(lists[1]), F.Copy))]
     wait("s", prev[0])
     syn.dma_start(T.y[:, 0:HALF], T.yo[0:128:16, 0:HALF]).then_inc(T.sem.d_y0, 16)
     wait("a", prev[1])
     act.dma_start(T.y[:, HALF:S], T.yo[0:128:16, HALF:S]).then_inc(T.sem.d_y1, 16)
-    if later:
-        g.wait_ge(T.sem.loc_k, nk)
-        g.wait_ge(T.sem.loc_l, nl)
-    syn.wait_ge(T.sem.d_y0, 16)
-    act.wait_ge(T.sem.d_y1, 16)
+    wait("g", ("loc", sent[0]))
+    wait("s", ("d_y0", 16))
+    wait("a", ("d_y1", 16))
+    for name in marks:
+        if name not in waited:
+            wait("s", (name, 1))

from concourse.bass import DstId, RemoteDMATransfer
from concourse.mybir import dt, AluOpType, AxisListType, ActivationFunctionType

NV = 8
S = 2048
Q = 512
HALF = S // 2
BW = 136
IDN = S + Q
BIG = float(3 * 2 ** 26)

JOIN = {
    2: (4, 5, 0, 64, "ca", "arrc0", [[7], [6, 5]]),
    3: (4, 5, 64, 64, "cb", "arrc1", [[7], [6, 5]]),
    1: (6, 7, 0, 128, "cf", "arrc2", [[7]]),
}

SCRATCH = {
    "lni": ("sbuf", [128, 64], "int32"),
    "fri": ("sbuf", [128, 64], "int32"),
    "liti": ("sbuf", [128, 32], "int32"),
    "litb": ("sbuf", [128, 32], "bfloat16"),
    "lnf": ("sbuf", [128, 64], "float32"),
    "zf": ("sbuf", [128, 64], "float32"),
    "stf": ("sbuf", [128, 72], "float32"),
    "exi": ("sbuf", [128, 72], "int32"),
    "dlt": ("sbuf", [128, 64], "float32"),
    "xx": ("sbuf", [128, 576], "bfloat16"),
    "iom": ("sbuf", [128, 136], "bfloat16"),
    "qm1": ("sbuf", [128, 32], "bfloat16"),
    "qm2": ("sbuf", [128, 32], "bfloat16"),
    "one": ("sbuf", [128, 144], "bfloat16"),
    "sele": ("sbuf", [128, 8], "bfloat16"),
    "selo": ("sbuf", [128, 8], "bfloat16"),
    "cneg": ("sbuf", [128, 128], "bfloat16"),
    "qrow": ("sbuf", [128, 128], "bfloat16"),
    "bcp": ("sbuf", [128, 4], "float32"),
    "bcn": ("sbuf", [128, 4], "float32"),
    "ap": ("sbuf", [128, 512], "bfloat16"),
    "am": ("sbuf", [128, 512], "bfloat16"),
    "bh": ("sbuf", [128, 4 * BW], "bfloat16"),
    "bl": ("sbuf", [128, 4 * BW], "bfloat16"),
    "wl": ("sbuf", [128, Q], "bfloat16"),
    "w0": ("sbuf", [128, S + Q], "bfloat16"),
    "w1": ("sbuf", [128, S + Q], "bfloat16"),
    "w2": ("sbuf", [128, S + Q], "bfloat16"),
    "w3": ("sbuf", [128, S + 2 * Q], "bfloat16"),
    "w5": ("sbuf", [128, S + 2 * Q], "bfloat16"),
    "yo": ("sbuf", [128, S], "float32"),
    "lland": ("dram", [NV, 128, 32], "bfloat16"),
    "pci": ("sbuf", [128, 8], "int32"),
    "p15": ("sbuf", [128, 8], "int32"),
    "h5": ("sbuf", [128, 4], "float32"),
    "h80": ("sbuf", [128, 4], "float32"),
    "pm0": ("sbuf", [128, 4], "float32"),
    "pm1": ("sbuf", [128, 4], "float32"),
    "lo": ("sbuf", [128, 160], "bfloat16"),
    "hib": ("sbuf", [128, 160], "bfloat16"),
    "hi": ("sbuf", [128, 160], "bfloat16"),
    "hix": ("sbuf", [128, 32], "bfloat16"),
    "d15": ("sbuf", [128, 144], "bfloat16"),
    "d14": ("sbuf", [128, 144], "bfloat16"),
    "e15": ("sbuf", [128, 144], "bfloat16"),
    "e14": ("sbuf", [128, 144], "bfloat16"),
    "ee": ("sbuf", [128, 144], "bfloat16"),
    "idw": ("sbuf", [128, IDN], "bfloat16"),
    "cw": ("sbuf", [128, S + Q], "bfloat16"),
    "cr": ("sbuf", [128, S], "bfloat16"),
    "ca": ("sbuf", [128, 64], "uint16"),
    "cb": ("sbuf", [128, 64], "uint16"),
    "cf": ("sbuf", [128, 128], "uint16"),
    "psm": ("psum", [128, 512], "float32"),
    "psq": ("psum", [128, 512], "float32"),
    "pdh": ("psum", [128, 512], "float32"),
    "pdl": ("psum", [128, 512], "float32"),
    "pout": ("psum", [128, 512], "float32"),
    "pjn": ("psum", [128, 512], "float32"),
}
for _v in range(NV):
    SCRATCH["ls%d" % _v] = ("sbuf", [128, 128], "uint16")

NOPS = 112
SEMAPHORES = (["d_ln", "d_fr", "d_li", "d_y0", "d_y1", "d_id", "d_cw", "loc", "arrc0", "arrc1", "arrc2"]
              + ["arrk%d" % v for v in range(NV - 1)] + ["arrl%d" % v for v in range(NV)]
              + ["lit%d" % v for v in range(NV)] + ["op%d" % k for k in range(NOPS)])


def rank_program(g, core, T, topo):
    r = T.rank_of(core)
    if r is None:
        return
    A = AluOpType
    F = ActivationFunctionType
    vec, act, pe, syn = g.vector, g.scalar, g.tensor, g.sync
    queues = {"g": g, "v": vec, "a": act, "p": pe, "s": syn}
    seen = {}
    waited = {}
    marks = []
    helper = r in JOIN

    def wait(q, *deps):
        for d in deps:
            if d is not None and (q, d) not in seen:
                seen[(q, d)] = True
                waited[d[0]] = True
                queues[q].wait_ge(T.sem[d[0]], d[1])

    def mark(ins):
        name = "op%d" % len(marks)
        marks.append(name)
        ins.then_inc(T.sem[name], 1)
        return (name, 1)

    def arrived(name, src):
        return (name, len(topo.engines(T.cores[src], core)))

    if r <= 4:
        stages = [[v] for v in range(r + 1)]
    else:
        stages = [[0], [1], [2], [3], [4, 5]] + ([[6]] if r == 6 else [[6, 7]] if r == 7 else [])
    wins = [T.wl] + [T["w%d" % st[-1]] for st in stages[:-1]]
    base = [0] + [S] * (len(stages) - 1)

    if r == 0:
        syn.dma_start(T.liti[:], T.lit[:]).then_inc(T.sem.d_li, 16)
        act.dma_start(T.lni[0:8, :], T.ln[:]).then_inc(T.sem.d_ln, 16)
        syn.dma_start(T.fri[0:8, :], T.frm[:]).then_inc(T.sem.d_fr, 16)
    else:
        syn.dma_start(T.lni[0:8, :], T.ln[:]).then_inc(T.sem.d_ln, 16)
        act.dma_start(T.fri[0:8, :], T.frm[:]).then_inc(T.sem.d_fr, 16)
        syn.dma_start(T.liti[:], T.lit[:]).then_inc(T.sem.d_li, 16)

    m_w = {}

    def zero_window(k):
        m_w[k] = mark(vec.memset(wins[k][:, base[k]:base[k] + Q * len(stages[k])], 0.0))

    m_one = mark(vec.memset(T.one[:], 1.0))
    if helper:
        m_id0 = mark(vec.memset(T.idw[:, 0:IDN // 2], 0.0))
    else:
        m_ap = mark(vec.memset(T.ap[:], 0.0))
    m_q1 = mark(vec.memset(T.qm1[:], -512.0))
    m_q2 = mark(vec.memset(T.qm2[:], 512.0))
    m_zf = mark(vec.memset(T.zf[0:8, :], 0.0))
    m_st = mark(vec.memset(T.stf[0:8, 0:1], -7.5))
    m_ex = mark(vec.memset(T.exi[0:8, 0:1], 0))
    m_neg = mark(vec.memset(T.cneg[0:1, :], -2048.0)) if r == 0 else None
    m_xx = mark(vec.memset(T.xx[0:8, :], 0.0))
    if helper:
        m_ap = mark(vec.memset(T.ap[:], 0.0))
        m_am = mark(vec.memset(T.am[:], 0.0))
    if r > 0:
        zero_window(0)
        zero_window(1)
    if helper:
        wait("a", m_id0)
        m_id1 = mark(act.activation(T.idw[:, IDN // 2:IDN], T.idw[:, 0:IDN // 2], F.Sigmoid, bias=-200.0))
    else:
        wait("a", m_ap)
        m_am = mark(act.activation(T.am[:], T.ap[:], F.Sigmoid, bias=-200.0))

    imp = {"allow_small_or_imprecise_dtypes": True}
    chain = [None]

    def gp(ins):
        chain[0] = mark(ins)
        return chain[0]

    wait("g", m_one)
    c_sele = gp(g.affine_select(T.sele[0:8, 0:4], T.one[0:8, 0:4], [[-2, 4]], A.is_equal, 0.0, 0, 1))
    wait("g", chain[0])
    c_selo = gp(g.affine_select(T.selo[0:8, 0:4], T.one[0:8, 0:4], [[-2, 4]], A.is_equal, 0.0, -1, 1))
    wait("g", chain[0])
    c_iom = gp(g.iota(T.iom[:, 0:129], [[16, 129]], -16, 0, **imp))
    wait("g", chain[0], m_q1)
    c_q1a = gp(g.iota(T.qm1[0:64, 0:16], [[1, 16]], -7, 0, **imp))
    wait("g", chain[0])
    c_q1b = gp(g.iota(T.qm1[64:128, 16:32], [[1, 16]], -7, 0, **imp))
    wait("g", chain[0], m_q2)
    c_q2a = gp(g.iota(T.qm2[0:64, 0:16], [[1, 16]], -7, 0, **imp))
    wait("g", chain[0])
    c_q2b = gp(g.iota(T.qm2[64:128, 16:32], [[1, 16]], -7, 0, **imp))
    wait("g", chain[0])
    c_qrow = gp(g.iota(T.qrow[0:1, :], [[0, 8], [1, 16]], 0, 0, **imp))
    if helper:
        wait("g", chain[0])
        c_pci = gp(g.iota(T.pci[:, 0:1], [[0, 1]], 0, 1))
        wait("g", chain[0])
        c_hib = gp(g.iota(T.hib[:], [[1, 5], [0, 32]], 0, 0, **imp))
        wait("g", chain[0])
        c_lo = gp(g.iota(T.lo[:], [[0, 5], [1, 32]], 0, 0, **imp))

    def xs(k):
        return T.xx[0:8, 64 + 128 * k:128 + 128 * k]

    if r == 0:
        wait("v", ("d_li", 16))
        o_lb = mark(vec.tensor_copy(T.litb[:], T.liti[:]))
    wait("v", ("d_ln", 16))
    o_lnf = mark(vec.tensor_copy(T.lnf[0:8, :], T.lni[0:8, :]))
    wait("v", ("d_fr", 16), m_ex)
    o_ex = mark(vec.tensor_tensor(T.exi[0:8, 1:65], T.fri[0:8, :], T.lni[0:8, :], A.add))
    wait("v", o_lnf, m_st, m_zf)
    o_st = mark(vec.tensor_tensor_scan(T.stf[0:8, 1:65], T.lnf[0:8, :], T.zf[0:8, :], -7.5, A.add, A.add))
    wait("v", o_ex, m_xx)
    o_xh = mark(vec.tensor_tensor(xs(1), T.fri[0:8, :], T.exi[0:8, 0:64], A.subtract))
    wait("v", o_st)
    o_xm = mark(vec.tensor_scalar(xs(0), T.stf[0:8, 0:64], BIG, -BIG, A.add, A.add))
    o_dl = mark(vec.tensor_tensor(T.dlt[0:8, :], T.fri[0:8, :], T.exi[0:8, 0:64], A.subtract))
    wait("v", o_xm)
    o_xq = mark(vec.tensor_tensor(xs(2), xs(0), T.stf[0:8, 0:64], A.subtract))
    wait("v", o_dl, o_xh)
    o_xl = mark(vec.tensor_tensor(xs(3), T.dlt[0:8, :], xs(1), A.subtract))
    if r > 0:
        wait("v", ("d_li", 16))
        o_lb = mark(vec.tensor_copy(T.litb[:], T.liti[:]))

    wait("p", c_iom, m_one)
    pe.matmul(T.pout[:, 0:128], T.one[0:1, 0:128], T.iom[0:1, 1:129], True, False)
    wait("p", c_sele, c_selo, m_xx)
    p_col = {}
    for ps, k, dep in (("pdh", 1, o_xh), ("psm", 0, o_xm), ("psq", 2, o_xq), ("pdl", 3, o_xl)):
        wait("p", dep)
        pe.matmul(T[ps][:, 0:4], T.xx[0:8, 64 + 128 * k:192 + 128 * k], T.sele[0:8, 0:4], True, False)
        p_col[ps] = mark(pe.matmul(T[ps][:, 0:4], T.xx[0:8, 128 * k:128 + 128 * k], T.selo[0:8, 0:4], False, True))
    wait("p", c_qrow, m_neg)
    pe.matmul(T.pout[:, 0:128], T.qrow[0:1, :], T.one[0:1, 0:128], False, False)
    if r == 0:
        pe.matmul(T.pout[:, 0:128], T.cneg[0:1, :], T.one[0:1, 0:128], False, False)

    wait("a", p_col["psq"])
    a_bp = mark(act.activation(T.bcp[:], T.psq[:, 0:4], F.Identity, scale=256.0))
    a_bn = mark(act.activation(T.bcn[:], T.psq[:, 0:4], F.Identity, scale=-256.0))
    wait("a", m_ap, m_am, c_q1a, c_q1b, c_q2a, c_q2b, a_bp, a_bn)
    a_lf = []
    for b in range(4):
        la = mark(act.activation(T.ap[:, 160 * b:160 * b + 32], T.qm1[:], F.Sigmoid, bias=T.bcp[:, b:b + 1], scale=256.0))
        lb = mark(act.activation(T.am[:, 160 * b:160 * b + 32], T.qm2[:], F.Sigmoid, bias=T.bcn[:, b:b + 1], scale=-256.0))
        a_lf.append((la, lb))
    v_b = []
    wait("v", c_iom, p_col["pdh"], p_col["psm"])
    for b in range(4):
        vh = mark(vec.tensor_scalar(T.bh[:, BW * b:BW * b + 129], T.iom[:, 0:129], T.psm[:, b:b + 1], T.pdh[:, b:b + 1],
                                    A.is_ge, A.mult))
        wait("v", p_col["pdl"])
        vl = mark(vec.tensor_scalar(T.bl[:, BW * b:BW * b + 129], T.iom[:, 0:129], T.psm[:, b:b + 1], T.pdl[:, b:b + 1],
                                    A.is_ge, A.mult))
        v_b.append((vh, vl))
    last = None
    for b in range(4):
        lp, lm = T.ap[:, 128 * b:128 * b + 128], T.am[:, 128 * b:128 * b + 128]
        now_h, now_l = T.bh[:, BW * b + 1:BW * b + 129], T.bl[:, BW * b + 1:BW * b + 129]
        old_h, old_l = T.bh[:, BW * b:BW * b + 128], T.bl[:, BW * b:BW * b + 128]
        wait("p", v_b[b][0], v_b[b][1], a_lf[b][0])
        pe.matmul(T.pout[:, 0:128], lp, now_h, False, False)
        pe.matmul(T.pout[:, 0:128], lp, now_l, False, False)
        wait("p", a_lf[b][1])
        pe.matmul(T.pout[:, 0:128], lm, old_h, False, False)
        last = pe.matmul(T.pout[:, 0:128], lm, old_l, False, b == 3)
    p_out = mark(last)
    if helper:
        wait("v", c_pci)
        o_p15 = mark(vec.tensor_scalar(T.p15[:, 0:1], T.pci[:, 0:1], 15, None, A.bitwise_and))
        wait("v", o_p15)
        o_h5 = mark(vec.tensor_scalar(T.h5[:, 0:1], T.p15[:, 0:1], 5.0, None, A.mult))
        o_h80 = mark(vec.tensor_scalar(T.h80[:, 0:1], T.p15[:, 0:1], 80.0, None, A.add))
    own = T["ls%d" % r]
    wait("v", p_out)
    o_ls = mark(vec.tensor_copy(own[:], T.pout[:, 0:128]))

    sent = [0]

    def send(src, dst, dests, sem):
        mask = topo.mask(core, T.cores[dests[0]])
        ids = []
        for d in dests:
            rid, pid, _se = topo.addr(T.cores[d])
            ids.append(DstId(rid=rid, pnc=pid))
        g.remote_dma_fused([RemoteDMATransfer(dst_ids=ids, dma_engine_mask=mask, remote_sem=T.sem[sem],
                                              srcs=[src], dsts=[dst] * len(dests))], local_sem=T.sem.loc)
        sent[0] += len(topo.engines(core, T.cores[dests[0]]))

    far = [d for d in range(NV - 1, r, -1) if d >= 4]
    near = [d for d in range(3, r, -1)]
    if far:
        wait("g", o_lb)
        send(T.litb[:], T.lland[r], far, "arrk%d" % r)
    if helper:
        wait("g", chain[0])
        c_d15 = gp(g.affine_select(T.d15[:], T.one[:], [[1, 144]], A.is_equal, 0.0, -15, -1))
        wait("g", chain[0])
        c_d14 = gp(g.affine_select(T.d14[:], T.one[:], [[1, 144]], A.is_equal, 0.0, -14, -1))
    wait("g", o_ls)
    if r <= 3:
        for c in ([[7], [6], [5, 4]] if r == 0 else [[7, 6], [5, 4]]):
            send(own[:], own[:], c, "arrl%d" % r)
    else:
        send(own[:], own[:], [h for h in JOIN if r in JOIN[h][0:2]], "arrl%d" % r)
    if near:
        send(T.litb[:], T.lland[r], near, "arrk%d" % r)
        send(own[:], own[:], near, "arrl%d" % r)

    if helper:
        wait("v", o_p15)
        o_pm0 = mark(vec.tensor_scalar(T.pm0[:, 0:1], T.p15[:, 0:1], 0.0, None, A.is_equal))
        o_pm1 = mark(vec.tensor_scalar(T.pm1[:, 0:1], T.p15[:, 0:1], 1.0, 32.0, A.is_equal, A.mult))
        m_cw = mark(vec.memset(T.cw[:, S:S + Q], 0.0))
    for k in range(len(stages)):
        if k not in m_w:
            zero_window(k)
    if helper:
        wait("v", c_d15, c_d14, o_pm0, o_pm1)
        o_e15 = mark(vec.tensor_scalar(T.e15[:], T.d15[:], T.pm0[:, 0:1], None, A.mult))
        o_e14 = mark(vec.tensor_scalar(T.e14[:], T.d14[:], T.pm1[:, 0:1], None, A.mult))
        wait("v", o_e15, o_e14)
        o_ee = mark(vec.tensor_tensor(T.ee[:], T.e15[:], T.e14[:], A.add))
        wait("a", c_hib, o_h5)
        a_hi = mark(act.activation(T.hi[:], T.hib[:], F.Identity, bias=T.h5[:, 0:1]))
        wait("a", o_h80, m_one)
        a_hix = mark(act.activation(T.hix[:], T.one[:, 0:32], F.Identity, scale=T.h80[:, 0:1]))
        wait("s", m_id0, m_id1, c_lo)
        syn.dma_start(T.idw[0:128:16, :], T.lo[:]).then_inc(T.sem.d_id, 16)
        wait("s", a_hi)
        syn.dma_start(T.idw[1:128:16, :], T.hi[:]).then_inc(T.sem.d_id, 16)
        wait("s", m_cw)
        syn.dma_start(T.cw[0:128:16, S:S + Q], T.lo[:, 0:32]).then_inc(T.sem.d_cw, 16)
        wait("s", a_hix)
        syn.dma_start(T.cw[1:128:16, S:S + Q], T.hix[:]).then_inc(T.sem.d_cw, 16)

    for k in range(len(stages)):
        for n, v in enumerate(stages[k]):
            at = base[k] + Q * n
            dst = wins[k][0:128:16, at:at + Q]
            wait("s", m_w[k])
            if v == r:
                wait("s", o_lb)
                syn.dma_start(dst, T.litb[:]).then_inc(T.sem["lit%d" % v], 16)
            else:
                wait("s", arrived("arrk%d" % v, v))
                syn.dma_start(dst, T.lland[v]).then_inc(T.sem["lit%d" % v], 16)

    if helper:
        v0, v1, c0, nc, buf, sem, calls = JOIN[r]
        l0, l1 = T["ls%d" % v0], T["ls%d" % v1]
        half = nc // 2
        for q in ("v", "a"):
            wait(q, ("d_id", 32), arrived("arrl%d" % v0, v0))
        i_v = mark(vec.tensor_copy(T.cw[:, 0:HALF], T.idw[:].indirect(l0[:, 0:64])))
        i_a = mark(act.activation(T.cw[:, HALF:S], T.idw[:].indirect(l0[:, 64:128]), F.Copy))
        for q in ("v", "a"):
            wait(q, i_v, i_a, ("d_cw", 32), arrived("arrl%d" % v1, v1))
        j_v = mark(vec.tensor_copy(T.cr[:, 0:16 * half], T.cw[:].indirect(l1[:, c0:c0 + half])))
        j_a = mark(act.activation(T.cr[:, 16 * half:16 * nc], T.cw[:].indirect(l1[:, c0 + half:c0 + nc]), F.Copy))
        wait("p", o_ee, j_v, j_a)
        for q in range(16):
            last = pe.matmul(T.pjn[:, 0:nc], T.ee[:, 15 - q:143 - q], T.cr[:, q:16 * nc:16], q == 0, q == 15)
        p_jn = mark(last)
        wait("v", p_jn)
        o_jn = mark(vec.tensor_copy(T[buf][:], T.pjn[:, 0:nc]))
        wait("g", o_jn)
        for c in calls:
            send(T[buf][:], T[buf][:], c, sem)

    prev = []
    for k, st in enumerate(stages):
        v = st[-1]
        win = wins[k][:, 0:base[k] + Q * len(st)]
        out = T.yo if k == len(stages) - 1 else wins[k + 1]
        if len(st) == 1:
            lst = T["ls%d" % v]
            lists = (lst[:, 0:64], lst[:, 64:128])
            got = [o_ls if v == r else arrived("arrl%d" % v, v)] * 2
        elif v == 5:
            lists = (T.ca[:], T.cb[:])
            got = [arrived("arrc0", 2), arrived("arrc1", 3)]
        else:
            lists = (T.cf[:, 0:64], T.cf[:, 64:128])
            got = [arrived("arrc2", 1)] * 2
        lits = [("lit%d" % x, 16) for x in st]
        wait("v", *lits, got[0], *prev)
        wait("a", *lits, got[1], *prev)
        prev = [mark(vec.tensor_copy(out[:, 0:HALF], win.indirect(lists[0]))),
                mark(act.activation(out[:, HALF:S], win.indirect(lists[1]), F.Copy))]
    wait("s", prev[0])
    syn.dma_start(T.y[:, 0:HALF], T.yo[0:128:16, 0:HALF]).then_inc(T.sem.d_y0, 16)
    wait("a", prev[1])
    act.dma_start(T.y[:, HALF:S], T.yo[0:128:16, HALF:S]).then_inc(T.sem.d_y1, 16)
    wait("g", ("loc", sent[0]))
    wait("s", ("d_y0", 16))
    wait("a", ("d_y1", 16))
    for name in marks:
        if name not in waited:
            wait("s", (name, 1))
